import numpy as np
import ml_dtypes


def mxq(x, axis, fmt="e4m3"):
    dtype, down = {"e4m3": (ml_dtypes.float8_e4m3fn, 7), "e5m2": (ml_dtypes.float8_e5m2, 14)}[fmt]
    v = np.moveaxis(np.asarray(x, np.float32).astype(ml_dtypes.bfloat16).astype(np.float64), axis, -1)
    blocks = v.reshape(v.shape[:-1] + (-1, 32))
    amax = np.abs(blocks).max(-1, keepdims=True)
    byte = np.maximum(np.where(amax > 0, np.frexp(amax)[1] - 1 + 127, 0) - down, 1)
    scale = np.exp2(byte - 127.0)
    codes = (blocks / scale).astype(np.float32).astype(dtype).astype(np.float64)
    return np.moveaxis((codes * scale).reshape(v.shape), -1, axis)


WIDE = False


def mx_kscale(k):
    if not WIDE:
        return np.ones(k)
    levels = np.array([10, -10, 5, -5, 0])
    if k % 512:
        return np.exp2(np.random.permutation(np.resize(levels, k // 32))).repeat(32)
    a = np.empty((k // 512, 16))
    for p in range(k // 512):
        a[p, :8] = np.random.permutation(np.resize(levels, 8))
        for g in range(8):
            far = levels[np.abs(levels - a[p, g]) >= 10]
            a[p, g + 8] = far[np.random.randint(len(far))]
    return np.exp2(a.ravel()).repeat(32)


def f64(x):
    return np.asarray(x).astype(np.float64)


def striped(idx):
    return np.tile(idx.reshape(-1, 16).T, (8, 1)).astype(np.uint16)


def unstriped(offs):
    return offs[:16].T.reshape(-1).astype(np.int64)


E2M1 = np.array([0.0, 0.5, 1.0, 1.5, 2.0, 3.0, 4.0, 6.0, -0.0, -0.5, -1.0, -1.5, -2.0, -3.0, -4.0, -6.0])


def pack_weight(w, fmt):
    k, n = w.shape
    w = f64(np.asarray(w, np.float32).astype(ml_dtypes.bfloat16)).reshape(k // 32, 32, n)
    amax = np.abs(w).max(1)
    if fmt == "e4m3":
        byte = np.frexp(amax)[1] - 1 + 127 - 7
    else:
        mant, ex = np.frexp(amax / 6.0)
        byte = np.where(mant > 0.5, ex, ex - 1) + 127
    byte = np.clip(np.where(amax > 0, byte, 1), 1, 254)
    scaled = (w * np.exp2(127.0 - byte)[:, None, :]).reshape(k, n).astype(np.float32)
    by_word = np.ascontiguousarray(scaled.reshape(k // 512, 128, 4, n).transpose(0, 1, 3, 2))
    if fmt == "e4m3":
        words = by_word.astype(ml_dtypes.float8_e4m3fn).view(np.uint8)
    else:
        c = by_word.astype(ml_dtypes.float4_e2m1fn).view(np.uint8) & 0xF
        words = (c[..., 0::2] | (c[..., 1::2] << 4)).reshape(k // 512, 128, 2 * n)
    return np.ascontiguousarray(words), np.ascontiguousarray(byte.astype(np.uint8).reshape(k // 512, 16, n))


def unpack_weight(words, scales, fmt):
    g, _, n = scales.shape
    words = np.ascontiguousarray(words).reshape(g, 128, n, -1)
    if fmt == "e4m3":
        vals = words.view(ml_dtypes.float8_e4m3fn).astype(np.float64)
    else:
        nib = np.empty((g, 128, n, 4), np.uint8)
        nib[..., 0::2] = words & 0xF
        nib[..., 1::2] = words >> 4
        vals = E2M1[nib]
    vals = vals * np.repeat(np.exp2(scales.astype(np.float64) - 127.0), 8, axis=1)[..., None]
    return vals.transpose(0, 1, 3, 2).reshape(g * 512, n)


def relu(v):
    return np.maximum(v, 0.0)


K, T, Q, E, C, D, H = 512, 512, 768, 6, 256, 128, 0
N, TOP = 512, 3


def by_expert(wq, xq, C):
    return np.concatenate([wq[e].T @ xq[:, e * C:(e + 1) * C] for e in range(E)], axis=1)


def setup_inputs():
    n = np.random.standard_normal
    s = mx_kscale(K)
    deal = np.repeat(np.arange(E), C).reshape(TOP, T)[:, np.random.permutation(T)]
    deal = np.take_along_axis(deal, np.argsort(np.random.rand(TOP, T), axis=0), axis=0)
    for _ in range(8):
        s_, t_ = np.random.permutation(T).reshape(2, -1); r = np.random.randint(TOP, size=T // 2); x, y = deal[r, s_].copy(), deal[r, t_].copy()
        ok = ~((deal[:, s_] == y).any(0) | (deal[:, t_] == x).any(0)); deal[r[ok], s_[ok]] = y[ok]; deal[r[ok], t_[ok]] = x[ok]
    order = np.lexsort((np.random.rand(TOP * T), deal.reshape(-1)))
    slot_token = order % T; pos = np.empty(TOP * T, np.int64); pos[order] = np.arange(TOP * T); pos = pos.reshape(TOP, T)
    g = np.random.uniform(0.5, 1.5, (TOP, T)); g = g / g.sum(0)
    slots2 = np.concatenate([np.random.permutation(Q)[:D] for e in range(E)])
    x = pack_weight(n((K, Q)) * s[:, None], "e4m3")
    return {
        "x_words": x[0],
        "x_scales": x[1],
        "xo": (n((K, T)) * s[:, None]).astype(np.float32),
        "w": (n((E, K, N)) / np.sqrt(K) / s[None, :, None]).astype(np.float32),
        "gate": np.stack([np.tile(r, (128, 1)) for r in g]).astype(np.float32),
        "offs": striped(slot_token),
        "pos1": striped(pos[0]),
        "pos2": striped(pos[1]),
        "pos3": striped(pos[2]),
        "offs2": striped(slots2),
    }


def reference(x_words, x_scales, xo, w, gate, offs, pos1, pos2, pos3, offs2):
    wq = mxq(f64(w), 1, "e4m3")
    idx, idx2 = unstriped(offs), unstriped(offs2)
    xq = mxq(f64(xo)[:, idx], 0, "e4m3")
    rq = unpack_weight(x_words, x_scales, "e4m3")[:, idx2]
    y = relu(by_expert(wq, xq, C))
    z = relu(by_expert(wq, rq, D))
    own = sum(f64(gate[r, :1]) * y[:, unstriped(p)] for r, p in enumerate((pos1, pos2, pos3)))
    return np.concatenate([own, z], axis=1)

@@ -1,0 +1,214 @@
+from contextlib import ExitStack
+
+import concourse.mybir as mybir
+
+F32 = mybir.dt.float32
+BF16 = mybir.dt.bfloat16
+I32 = mybir.dt.int32
+U32 = mybir.dt.uint32
+U16 = mybir.dt.uint16
+U8 = mybir.dt.uint8
+FP8X4 = mybir.dt.float8_e4m3fn_x4
+RELU = mybir.ActivationFunctionType.Relu
+MULT = mybir.AluOpType.mult
+ADD = mybir.AluOpType.add
+
+K, T, Q, E, C, D, N, TOP = 512, 512, 768, 6, 256, 128, 512, 3
+P = 128
+PACK = 4
+S = E * C
+R = E * D
+HALF = N // 2
+CHUNKS = N // P
+BANK = 512
+
+FLOPS = 2 * K * N * (S + R)
+
+
+def tile_moe_loc_lin_relu_kernel(
+    tc, x_words, x_scales, xo, w, gate, offs, pos1, pos2, pos3, offs2, out
+):
+    nc = tc.nc
+    with ExitStack() as ctx:
+        keep = ctx.enter_context(tc.tile_pool(name="keep", bufs=1))
+        ring = ctx.enter_context(tc.tile_pool(name="ring", bufs=3))
+        psum_y = ctx.enter_context(tc.psum_pool(name="psum_y", bufs=6))
+        psum_z = ctx.enter_context(tc.psum_pool(name="psum_z", bufs=2))
+
+        def load_list(src, name):
+            tile = keep.tile([P, src.shape[1]], U16, name=name)
+            nc.sync.dma_start(tile[:], src)
+            return tile
+
+        warm = keep.tile([P, 8], F32, name="warm")
+        nc.vector.memset(warm[:, 0:1], 0.0)
+        nc.scalar.activation(warm[:, 4:5], warm[:, 0:1], RELU)
+
+        far_scale_table = keep.tile([P, Q], U8, name="far_scale_table")
+        nc.gpsimd.memset(far_scale_table[:].bitcast(I32), 0)
+        far_list = load_list(offs2, "far_list")
+        far_word_table = keep.tile([P, Q], I32, name="far_word_table")
+        nc.sync.dma_start(far_word_table[:], x_words[0].rearrange("p t d -> p (t d)").bitcast(I32))
+        for q in range(4):
+            nc.sync.dma_start(
+                far_scale_table[32 * q : 32 * q + 4, :].bitcast(I32), x_scales[0, 4 * q : 4 * q + 4, :].bitcast(I32)
+            )
+        xo_rows = xo.rearrange("(p j) t -> p j t", j=PACK)
+        xo_raw = [keep.tile([P, 2, T], F32, name=f"xo_raw{u}") for u in range(2)]
+        nc.sync.dma_start(xo_raw[0][:], xo_rows[:, 0:2, :])
+        own_list = load_list(offs, "own_list")
+        nc.sync.dma_start(xo_raw[1][:], xo_rows[:, 2:4, :])
+
+        w_raw = {}
+
+        def load_w(e, h):
+            w_raw[e, h] = keep.tile([P, PACK, HALF], F32, name=f"w_raw{e}_{h}")
+            nc.sync.dma_start(w_raw[e, h][:], w[e].rearrange("(p j) n -> p j n", j=PACK)[:, :, HALF * h : HALF * (h + 1)])
+
+        for e in range(E):
+            load_w(e, 0)
+        slot_lists = [load_list(src, f"slot_list{r}") for r, src in enumerate((pos1, pos2, pos3))]
+        gates = keep.tile([P, TOP, T], F32, name="gates")
+        for e in range(2):
+            load_w(e, 1)
+        nc.sync.dma_start(gates[:], gate.rearrange("r p t -> p r t"))
+        for e in range(2, E):
+            load_w(e, 1)
+
+        pairs = [keep.tile([P, 2 * T], BF16, name=f"pairs{u}") for u in range(2)]
+        picked = keep.tile([P, 2, 2 * S], BF16, name="picked")
+        own_codes = keep.tile([P, S], U32, name="own_codes", align_bytes=64)
+        own_scales = keep.tile([P, S], U8, name="own_scales", align_bytes=64)
+        far_codes = keep.tile([P, R], U32, name="far_codes", align_bytes=64)
+        far_scales = keep.tile([P, R], U8, name="far_scales", align_bytes=64)
+        w_codes = keep.tile([P, E, N], U32, name="w_codes", align_bytes=64)
+        w_scales = keep.tile([P, E, N], U8, name="w_scales", align_bytes=64)
+        y = [keep.tile([P, S], F32, name=f"y{c}") for c in range(CHUNKS)]
+        z = [keep.tile([P, 2, R], F32, name=f"z{h}") for h in range(2)]
+
+        def gather_far(dst, table, i):
+            a = i * R // 2
+            nc.vector.tensor_copy(dst[:, a : a + R // 2], table.indirect(far_list[:, a // 16 : (a + R // 2) // 16]))
+
+        def round_tokens(u):
+            nc.scalar.copy(pairs[u][:].rearrange("p (t e) -> p t e", e=2), xo_raw[u][:].rearrange("p e t -> p t e"))
+
+        def gather_own(u, e):
+            nc.vector.tensor_copy(
+                picked[:, u, 2 * C * e : 2 * C * (e + 1)].bitcast(U32),
+                pairs[u][:].bitcast(U32).indirect(own_list[:, e * C // 16 : (e + 1) * C // 16]),
+            )
+
+        grouped = [keep.tile([P, PACK * BANK], BF16, name=f"grouped{g}", align_bytes=64) for g in range(E // 2)]
+        w_grouped = {}
+
+        def interleave_own(g):
+            nc.vector.tensor_copy(
+                grouped[g][:].rearrange("p (s u e) -> p s u e", u=2, e=2),
+                picked[:, :, 2 * BANK * g : 2 * BANK * (g + 1)].rearrange("p u (s e) -> p s u e", e=2),
+            )
+
+        def quantize_own(g):
+            cols = slice(BANK * g, BANK * (g + 1))
+            nc.vector.quantize_mx(out=own_codes[:, cols].bitcast(FP8X4), scales=own_scales[:, cols], in_=grouped[g][:])
+
+        def round_w(e, h):
+            w_grouped[e, h] = keep.tile([P, PACK * HALF], BF16, name=f"w_grouped{e}_{h}", align_bytes=64)
+            nc.scalar.copy(
+                w_grouped[e, h][:].rearrange("p (c i j) -> p c j i", i=4, j=PACK),
+                w_raw[e, h][:].rearrange("p j (c i) -> p c j i", i=4),
+            )
+
+        def quantize_w(e, h):
+            cols = slice(HALF * h, HALF * (h + 1))
+            nc.vector.quantize_mx(
+                out=w_codes[:, e, cols].bitcast(FP8X4), scales=w_scales[:, e, cols], in_=w_grouped[e, h][:]
+            )
+
+        def product(dst, e, c, codes, scales):
+            cols = slice(P * c, P * (c + 1))
+            nc.tensor.matmul_mx(
+                out=dst,
+                lhsT=w_codes[:, e, cols].bitcast(FP8X4),
+                lhsT_scale=w_scales[:, e, cols],
+                rhs=codes.bitcast(FP8X4),
+                rhs_scale=scales,
+                start=True,
+                stop=True,
+            )
+
+        def own_results(c, g):
+            acc = psum_y.tile([P, BANK], F32, name="acc_y")
+            for i in range(2):
+                e = 2 * g + i
+                slots = slice(C * e, C * (e + 1))
+                product(acc[:, C * i : C * (i + 1)], e, c, own_codes[:, slots], own_scales[:, slots])
+            nc.scalar.activation(y[c][:, BANK * g : BANK * (g + 1)], acc[:], RELU)
+
+        def far_results(h, g):
+            acc = psum_z.tile([P, 2, 2 * D], F32, name="acc_z")
+            for k in range(2):
+                for i in range(2):
+                    e = 2 * g + i
+                    slots = slice(D * e, D * (e + 1))
+                    product(acc[:, k, D * i : D * (i + 1)], e, 2 * h + k, far_codes[:, slots], far_scales[:, slots])
+            nc.scalar.activation(z[h][:, :, 2 * D * g : 2 * D * (g + 1)], acc[:], RELU)
+
+        def store_far(h):
+            for k in range(2):
+                c = 2 * h + k
+                nc.sync.dma_start(out[P * c : P * (c + 1), T:], z[h][:, k, :])
+
+        def combine(c):
+            terms = [ring.tile([P, T], F32, name=f"term{r}") for r in range(TOP)]
+            for r in range(TOP):
+                nc.vector.tensor_tensor(terms[r][:], y[c][:].indirect(slot_lists[r][:]), gates[:, r, :], MULT)
+            partial = ring.tile([P, T], F32, name="partial")
+            nc.vector.tensor_tensor(partial[:], terms[0][:], terms[1][:], ADD)
+            total = ring.tile([P, T], F32, name="total")
+            nc.vector.tensor_tensor(total[:], partial[:], terms[2][:], ADD)
+            nc.sync.dma_start(out[P * c : P * (c + 1), 0:T], total[:])
+
+        for u in range(2):
+            round_tokens(u)
+        for i in range(2):
+            gather_far(far_codes, far_word_table[:].bitcast(U32), i)
+        gather_far(far_scales, far_scale_table[:], 0)
+        for e in range(E):
+            round_w(e, 0)
+        for g in range(E // 2):
+            for e in (2 * g, 2 * g + 1):
+                gather_own(0, e)
+            if g > 0:
+                quantize_w(3 * g - 1, 0)
+            for e in (2 * g, 2 * g + 1):
+                gather_own(1, e)
+            interleave_own(g)
+            if g < 2:
+                quantize_w(3 * g, 0)
+                quantize_own(g)
+                quantize_w(3 * g + 1, 0)
+            else:
+                round_w(0, 1)
+                round_w(1, 1)
+                quantize_w(0, 1)
+                quantize_own(g)
+            for c in range(2):
+                own_results(c, g)
+        gather_far(far_scales, far_scale_table[:], 1)
+        quantize_w(1, 1)
+        for e in range(2, E):
+            round_w(e, 1)
+        combine(0)
+        for e in range(2, E):
+            quantize_w(e, 1)
+        combine(1)
+        for c in range(2, CHUNKS):
+            for g in range(E // 2):
+                own_results(c, g)
+        for h in range(2):
+            for g in range(E // 2):
+                far_results(h, g)
+            store_far(h)
+        for c in range(2, CHUNKS):
+            combine(c)

@@ -1,6 +1,7 @@
 from contextlib import ExitStack
 
 import concourse.mybir as mybir
+from concourse.masks import make_identity
 
 F32 = mybir.dt.float32
 BF16 = mybir.dt.bfloat16
@@ -21,6 +22,7 @@ R = E * D
 HALF = N // 2
 CHUNKS = N // P
 BANK = 512
+WINDOW = 1024
 
 FLOPS = 2 * K * N * (S + R)
 
@@ -31,106 +33,142 @@ def tile_moe_loc_lin_relu_kernel(
     nc = tc.nc
     with ExitStack() as ctx:
         keep = ctx.enter_context(tc.tile_pool(name="keep", bufs=1))
-        ring = ctx.enter_context(tc.tile_pool(name="ring", bufs=3))
-        psum_y = ctx.enter_context(tc.psum_pool(name="psum_y", bufs=6))
-        psum_z = ctx.enter_context(tc.psum_pool(name="psum_z", bufs=2))
+        reuse = ctx.enter_context(tc.tile_pool(name="reuse", bufs=1))
+        psum = ctx.enter_context(tc.psum_pool(name="psum", bufs=1))
+        banks = [psum.tile([P, BANK], F32, name=f"bank{b}") for b in range(8)]
+        identity = keep.tile([P, P], F32, name="identity")
 
         def load_list(src, name):
             tile = keep.tile([P, src.shape[1]], U16, name=name)
             nc.sync.dma_start(tile[:], src)
             return tile
 
-        warm = keep.tile([P, 8], F32, name="warm")
-        nc.vector.memset(warm[:, 0:1], 0.0)
-        nc.scalar.activation(warm[:, 4:5], warm[:, 0:1], RELU)
-
-        far_scale_table = keep.tile([P, Q], U8, name="far_scale_table")
+        far_scale_table = keep.tile([P, WINDOW], U8, name="far_scale_table")
         nc.gpsimd.memset(far_scale_table[:].bitcast(I32), 0)
-        far_list = load_list(offs2, "far_list")
-        far_word_table = keep.tile([P, Q], I32, name="far_word_table")
-        nc.sync.dma_start(far_word_table[:], x_words[0].rearrange("p t d -> p (t d)").bitcast(I32))
-        for q in range(4):
-            nc.sync.dma_start(
-                far_scale_table[32 * q : 32 * q + 4, :].bitcast(I32), x_scales[0, 4 * q : 4 * q + 4, :].bitcast(I32)
-            )
+        warm = keep.tile([P, 16], F32, name="warm")
+        nc.gpsimd.memset(warm[:, 0:1], 0.0)
+        far_word_table = keep.tile([P, WINDOW], I32, name="far_word_table")
+        nc.gpsimd.memset(far_word_table[:, Q:], 0)
+        pairs = [keep.tile([P, 2 * WINDOW], BF16, name=f"pairs{u}") for u in range(2)]
+        for u in range(2):
+            nc.gpsimd.memset(pairs[u][:, 2 * T :].bitcast(I32), 0)
+        make_identity(nc, identity[:])
         xo_rows = xo.rearrange("(p j) t -> p j t", j=PACK)
         xo_raw = [keep.tile([P, 2, T], F32, name=f"xo_raw{u}") for u in range(2)]
+        w_raw = {}
+        whole_raw = [keep.tile([P, PACK, N], F32, name=f"whole_raw{e}") for e in range(3)]
+        for e in range(3):
+            for h in range(2):
+                w_raw[e, h] = whole_raw[e][:, :, HALF * h : HALF * (h + 1)]
+        placed = {(5, 0): 5632, (5, 1): 15360 + 4096}
+        for e in range(3, E):
+            for h in range(2):
+                if (e, h) in placed:
+                    w_raw[e, h] = reuse.tile([P, PACK, HALF], F32, name=f"w_raw{e}_{h}", offset=placed[e, h])[:]
+                else:
+                    w_raw[e, h] = keep.tile([P, PACK, HALF], F32, name=f"w_raw{e}_{h}")[:]
+
+        def w_rows(e):
+            return w[e].rearrange("(p j) n -> p j n", j=PACK)
+
+        def load_scale_rows(q):
+            nc.sync.dma_start(
+                far_scale_table[32 * q : 32 * q + 4, :Q].bitcast(I32), x_scales[0, 4 * q : 4 * q + 4, :].bitcast(I32)
+            )
+
+        def load_half(e, h):
+            nc.sync.dma_start(w_raw[e, h], w_rows(e)[:, :, HALF * h : HALF * (h + 1)])
+
+        nc.scalar.activation(warm[:, 8:9], warm[:, 0:1], RELU)
+        nc.sync.dma_start(far_word_table[:, :Q], x_words[0].rearrange("p t d -> p (t d)").bitcast(I32))
+        far_list = load_list(offs2, "far_list")
         nc.sync.dma_start(xo_raw[0][:], xo_rows[:, 0:2, :])
         own_list = load_list(offs, "own_list")
         nc.sync.dma_start(xo_raw[1][:], xo_rows[:, 2:4, :])
-
-        w_raw = {}
-
-        def load_w(e, h):
-            w_raw[e, h] = keep.tile([P, PACK, HALF], F32, name=f"w_raw{e}_{h}")
-            nc.sync.dma_start(w_raw[e, h][:], w[e].rearrange("(p j) n -> p j n", j=PACK)[:, :, HALF * h : HALF * (h + 1)])
-
-        for e in range(E):
-            load_w(e, 0)
+        load_half(3, 0)
+        nc.sync.dma_start(whole_raw[2][:], w_rows(2))
+        load_scale_rows(0)
+        load_scale_rows(1)
+        nc.sync.dma_start(whole_raw[0][:], w_rows(0))
+        load_scale_rows(2)
+        load_scale_rows(3)
+        nc.sync.dma_start(whole_raw[1][:], w_rows(1))
         slot_lists = [load_list(src, f"slot_list{r}") for r, src in enumerate((pos1, pos2, pos3))]
+        load_half(4, 0)
+        load_half(5, 0)
         gates = keep.tile([P, TOP, T], F32, name="gates")
-        for e in range(2):
-            load_w(e, 1)
         nc.sync.dma_start(gates[:], gate.rearrange("r p t -> p r t"))
-        for e in range(2, E):
-            load_w(e, 1)
+        load_half(3, 1)
+        load_half(4, 1)
+        load_half(5, 1)
 
-        pairs = [keep.tile([P, 2 * T], BF16, name=f"pairs{u}") for u in range(2)]
         picked = keep.tile([P, 2, 2 * S], BF16, name="picked")
         own_codes = keep.tile([P, S], U32, name="own_codes", align_bytes=64)
         own_scales = keep.tile([P, S], U8, name="own_scales", align_bytes=64)
         far_codes = keep.tile([P, R], U32, name="far_codes", align_bytes=64)
-        far_scales = keep.tile([P, R], U8, name="far_scales", align_bytes=64)
-        w_codes = keep.tile([P, E, N], U32, name="w_codes", align_bytes=64)
-        w_scales = keep.tile([P, E, N], U8, name="w_scales", align_bytes=64)
-        y = [keep.tile([P, S], F32, name=f"y{c}") for c in range(CHUNKS)]
+        far_scales = reuse.tile([P, R], U8, name="far_scales", offset=6144, align_bytes=64)
+        w_codes = [keep.tile([P, E * HALF], U32, name=f"w_codes{h}", align_bytes=64) for h in range(2)]
+        w_scales = [keep.tile([P, E * HALF], U8, name=f"w_scales{h}", align_bytes=64) for h in range(2)]
+        y = [reuse.tile([P, S], F32, name=f"y{c}", offset=at) for c, at in enumerate((0, 9216, 15360, 21504))]
         z = [keep.tile([P, 2, R], F32, name=f"z{h}") for h in range(2)]
 
-        def gather_far(dst, table, i):
-            a = i * R // 2
-            nc.vector.tensor_copy(dst[:, a : a + R // 2], table.indirect(far_list[:, a // 16 : (a + R // 2) // 16]))
+        def gather_far(dst, table, a, b):
+            nc.vector.tensor_copy(dst, table.indirect(far_list[:, a // 16 : b // 16]))
 
         def round_tokens(u):
-            nc.scalar.copy(pairs[u][:].rearrange("p (t e) -> p t e", e=2), xo_raw[u][:].rearrange("p e t -> p t e"))
-
-        def gather_own(u, e):
-            nc.vector.tensor_copy(
-                picked[:, u, 2 * C * e : 2 * C * (e + 1)].bitcast(U32),
-                pairs[u][:].bitcast(U32).indirect(own_list[:, e * C // 16 : (e + 1) * C // 16]),
+            nc.scalar.copy(
+                pairs[u][:, : 2 * T].rearrange("p (t e) -> p t e", e=2), xo_raw[u][:].rearrange("p e t -> p t e")
             )
 
-        grouped = [keep.tile([P, PACK * BANK], BF16, name=f"grouped{g}", align_bytes=64) for g in range(E // 2)]
+        def gather_own(u, g):
+            nc.vector.tensor_copy(
+                picked[:, u, 2 * BANK * g : 2 * BANK * (g + 1)].bitcast(U32),
+                pairs[u][:].bitcast(U32).indirect(own_list[:, g * BANK // 16 : (g + 1) * BANK // 16]),
+            )
+
+        grouped = keep.tile([P, PACK * S], BF16, name="grouped", align_bytes=64)
         w_grouped = {}
+        for h in range(2):
+            for g in range(E // 2):
+                at = 27648 if (h, g) == (1, 2) else None
+                pool = keep if at is None else reuse
+                w_grouped[h, g] = pool.tile([P, 2 * PACK * HALF], BF16, name=f"w_grouped{h}_{g}", align_bytes=64, offset=at)
 
         def interleave_own(g):
             nc.vector.tensor_copy(
-                grouped[g][:].rearrange("p (s u e) -> p s u e", u=2, e=2),
-                picked[:, :, 2 * BANK * g : 2 * BANK * (g + 1)].rearrange("p u (s e) -> p s u e", e=2),
+                grouped[:, PACK * BANK * g : PACK * BANK * (g + 1)].bitcast(I32).rearrange("p (s u) -> p s u", u=2),
+                picked[:, :, 2 * BANK * g : 2 * BANK * (g + 1)].bitcast(I32).rearrange("p u s -> p s u"),
             )
 
         def quantize_own(g):
             cols = slice(BANK * g, BANK * (g + 1))
-            nc.vector.quantize_mx(out=own_codes[:, cols].bitcast(FP8X4), scales=own_scales[:, cols], in_=grouped[g][:])
-
-        def round_w(e, h):
-            w_grouped[e, h] = keep.tile([P, PACK * HALF], BF16, name=f"w_grouped{e}_{h}", align_bytes=64)
-            nc.scalar.copy(
-                w_grouped[e, h][:].rearrange("p (c i j) -> p c j i", i=4, j=PACK),
-                w_raw[e, h][:].rearrange("p j (c i) -> p c j i", i=4),
+            nc.vector.quantize_mx(
+                out=own_codes[:, cols].bitcast(FP8X4),
+                scales=own_scales[:, cols],
+                in_=grouped[:, PACK * BANK * g : PACK * BANK * (g + 1)],
             )
 
-        def quantize_w(e, h):
-            cols = slice(HALF * h, HALF * (h + 1))
+        def round_w(e, h):
+            nc.scalar.copy(
+                w_grouped[h, e // 2][:, PACK * HALF * (e % 2) : PACK * HALF * (e % 2 + 1)].rearrange("p (c i j) -> p c j i", i=4, j=PACK),
+                w_raw[e, h].rearrange("p j (c i) -> p c j i", i=4),
+            )
+
+        def quantize_w(h, g):
+            cols = slice(2 * HALF * g, 2 * HALF * (g + 1))
             nc.vector.quantize_mx(
-                out=w_codes[:, e, cols].bitcast(FP8X4), scales=w_scales[:, e, cols], in_=w_grouped[e, h][:]
+                out=w_codes[h][:, cols].bitcast(FP8X4),
+                scales=w_scales[h][:, cols],
+                in_=w_grouped[h, g][:],
             )
 
         def product(dst, e, c, codes, scales):
-            cols = slice(P * c, P * (c + 1))
+            h, k = divmod(c, 2)
+            cols = slice(HALF * e + P * k, HALF * e + P * (k + 1))
             nc.tensor.matmul_mx(
                 out=dst,
-                lhsT=w_codes[:, e, cols].bitcast(FP8X4),
-                lhsT_scale=w_scales[:, e, cols],
+                lhsT=w_codes[h][:, cols].bitcast(FP8X4),
+                lhsT_scale=w_scales[h][:, cols],
                 rhs=codes.bitcast(FP8X4),
                 rhs_scale=scales,
                 start=True,
@@ -138,7 +176,7 @@ def tile_moe_loc_lin_relu_kernel(
             )
 
         def own_results(c, g):
-            acc = psum_y.tile([P, BANK], F32, name="acc_y")
+            acc = banks[3 * (c % 2) + g]
             for i in range(2):
                 e = 2 * g + i
                 slots = slice(C * e, C * (e + 1))
@@ -146,69 +184,106 @@ def tile_moe_loc_lin_relu_kernel(
             nc.scalar.activation(y[c][:, BANK * g : BANK * (g + 1)], acc[:], RELU)
 
         def far_results(h, g):
-            acc = psum_z.tile([P, 2, 2 * D], F32, name="acc_z")
+            acc = banks[(6 + 3 * h + g) % 8][:].rearrange("p (k s) -> p k s", k=2)
             for k in range(2):
                 for i in range(2):
                     e = 2 * g + i
                     slots = slice(D * e, D * (e + 1))
                     product(acc[:, k, D * i : D * (i + 1)], e, 2 * h + k, far_codes[:, slots], far_scales[:, slots])
-            nc.scalar.activation(z[h][:, :, 2 * D * g : 2 * D * (g + 1)], acc[:], RELU)
+            nc.scalar.activation(z[h][:, :, 2 * D * g : 2 * D * (g + 1)], acc, RELU)
 
         def store_far(h):
             for k in range(2):
                 c = 2 * h + k
                 nc.sync.dma_start(out[P * c : P * (c + 1), T:], z[h][:, k, :])
 
-        def combine(c):
-            terms = [ring.tile([P, T], F32, name=f"term{r}") for r in range(TOP)]
+        def weighted(c, cols):
+            width = cols.stop - cols.start
+            terms = []
             for r in range(TOP):
-                nc.vector.tensor_tensor(terms[r][:], y[c][:].indirect(slot_lists[r][:]), gates[:, r, :], MULT)
-            partial = ring.tile([P, T], F32, name="partial")
-            nc.vector.tensor_tensor(partial[:], terms[0][:], terms[1][:], ADD)
-            total = ring.tile([P, T], F32, name="total")
-            nc.vector.tensor_tensor(total[:], partial[:], terms[2][:], ADD)
-            nc.sync.dma_start(out[P * c : P * (c + 1), 0:T], total[:])
+                at = 27648 + 2048 * (r - 1) if c == 1 and r > 0 else None
+                pool = keep if at is None else reuse
+                term = pool.tile([P, width], F32, name=f"term{c}_{r}_{cols.start}", offset=at)
+                offsets = slot_lists[r][:, cols.start // 16 : cols.stop // 16]
+                nc.vector.tensor_tensor(term[:], y[c][:].indirect(offsets), gates[:, r, cols], MULT)
+                terms.append(term)
+            return terms
+
+        totals = [keep.tile([P, T], F32, name=f"total{c}") for c in range(CHUNKS)]
+        staged = [keep.tile([P, T], F32, name=f"staged{c}") for c in range(CHUNKS)]
+
+        def turn_and_add(c, terms, bank):
+            width = terms[0].shape[1]
+            for b in range(0, width, P):
+                for r in range(TOP):
+                    nc.tensor.matmul(
+                        bank[:, b : b + P],
+                        lhsT=terms[r][:, b : b + P],
+                        rhs=identity[:],
+                        start=r == 0,
+                        stop=r == TOP - 1,
+                        is_transpose=True,
+                    )
+            nc.scalar.copy(staged[c][:, :width], bank[:, :width])
+
+        def turn_back(c, width, bank):
+            for b in range(0, width, P):
+                nc.tensor.transpose(bank[:, b : b + P], staged[c][:, b : b + P], identity[:])
+            nc.scalar.copy(totals[c][:, :width], bank[:, :width])
+
+        def store_own(c):
+            nc.sync.dma_start(out[P * c : P * (c + 1), :T], totals[c][:])
 
         for u in range(2):
             round_tokens(u)
-        for i in range(2):
-            gather_far(far_codes, far_word_table[:].bitcast(U32), i)
-        gather_far(far_scales, far_scale_table[:], 0)
-        for e in range(E):
-            round_w(e, 0)
-        for g in range(E // 2):
-            for e in (2 * g, 2 * g + 1):
-                gather_own(0, e)
-            if g > 0:
-                quantize_w(3 * g - 1, 0)
-            for e in (2 * g, 2 * g + 1):
-                gather_own(1, e)
-            interleave_own(g)
-            if g < 2:
-                quantize_w(3 * g, 0)
-                quantize_own(g)
-                quantize_w(3 * g + 1, 0)
-            else:
-                round_w(0, 1)
-                round_w(1, 1)
-                quantize_w(0, 1)
-                quantize_own(g)
-            for c in range(2):
-                own_results(c, g)
-        gather_far(far_scales, far_scale_table[:], 1)
-        quantize_w(1, 1)
-        for e in range(2, E):
+        for e, h in ((3, 0), (2, 0), (2, 1), (0, 0), (0, 1), (1, 0), (1, 1), (4, 0), (5, 0)):
+            round_w(e, h)
+        gather_far(far_codes[:], far_word_table[:].bitcast(U32), 0, R)
+        gather_own(0, 0)
+        gather_own(1, 0)
+        gather_own(0, 1)
+        interleave_own(0)
+        gather_own(1, 1)
+        quantize_own(0)
+        gather_own(0, 2)
+        interleave_own(1)
+        gather_own(1, 2)
+        quantize_own(1)
+        interleave_own(2)
+        quantize_w(0, 0)
+        quantize_own(2)
+        for g in range(1, E // 2):
+            quantize_w(0, g)
+        gather_far(far_scales[:], far_scale_table[:], 0, R)
+        for c, g in ((0, 1), (0, 0), (0, 2), (1, 1), (1, 0)):
+            own_results(c, g)
+        for e in range(3, E - 1):
             round_w(e, 1)
-        combine(0)
-        for e in range(2, E):
-            quantize_w(e, 1)
-        combine(1)
-        for c in range(2, CHUNKS):
-            for g in range(E // 2):
-                own_results(c, g)
+        own_results(1, 2)
+        round_w(E - 1, 1)
+        for g in range(E // 2):
+            quantize_w(1, g)
+        for c, g in ((2, 0), (2, 1), (3, 0), (3, 1), (2, 2), (3, 2)):
+            own_results(c, g)
         for h in range(2):
             for g in range(E // 2):
                 far_results(h, g)
             store_far(h)
-        for c in range(2, CHUNKS):
-            combine(c)
+        terms = [weighted(c, slice(0, T)) for c in range(CHUNKS - 1)]
+        terms.append(weighted(CHUNKS - 1, slice(0, T // 2)))
+        last = weighted(CHUNKS - 1, slice(T // 2, T))
+        turn_and_add(0, terms[0], banks[4])
+        turn_and_add(1, terms[1], banks[5])
+        turn_back(0, T, banks[6])
+        store_own(0)
+        turn_back(1, T, banks[7])
+        store_own(1)
+        turn_and_add(2, terms[2], banks[4])
+        turn_and_add(3, terms[3], banks[5])
+        turn_back(2, T, banks[2])
+        store_own(2)
+        turn_back(3, T // 2, banks[3])
+        partial = keep.tile([P, T // 2], F32, name="partial")
+        nc.vector.tensor_tensor(partial[:], last[0][:], last[1][:], ADD)
+        nc.vector.tensor_tensor(totals[3][:, T // 2 :], partial[:], last[2][:], ADD)
+        store_own(3)

@@ -10,21 +10,33 @@ U32 = mybir.dt.uint32
 U16 = mybir.dt.uint16
 U8 = mybir.dt.uint8
 FP8X4 = mybir.dt.float8_e4m3fn_x4
+COPY = mybir.ActivationFunctionType.Copy
 RELU = mybir.ActivationFunctionType.Relu
 MULT = mybir.AluOpType.mult
 ADD = mybir.AluOpType.add
 
-K, T, Q, E, C, D, N, TOP = 512, 512, 768, 6, 256, 128, 512, 3
+K, N, EXPERTS, TOP = 512, 512, 6, 3
+OWN_TOKENS, FAR_TOKENS = 512, 768
+OWN_PER_EXPERT, FAR_PER_EXPERT = 256, 128
+OWN_SLOTS, FAR_SLOTS = EXPERTS * OWN_PER_EXPERT, EXPERTS * FAR_PER_EXPERT
 P = 128
 PACK = 4
-S = E * C
-R = E * D
-HALF = N // 2
 CHUNKS = N // P
+HALF = N // 2
+PAIRS = EXPERTS // 2
 BANK = 512
 WINDOW = 1024
+WHOLE_EXPERTS = 2
 
-FLOPS = 2 * K * N * (S + R)
+RESULT_BYTES = 4 * OWN_SLOTS
+SCALE_GAP = 3072
+RESULT_AT = (0, RESULT_BYTES + SCALE_GAP, 2 * RESULT_BYTES + SCALE_GAP, 3 * RESULT_BYTES + SCALE_GAP)
+FAR_SCALES_AT = RESULT_BYTES
+LAST_RAW_AT = (RESULT_BYTES - 512, RESULT_AT[3] - 2048)
+LAST_ROUNDED_AT = RESULT_AT[3] + RESULT_BYTES
+PARTIAL_AT = LAST_ROUNDED_AT + 4096
+
+FLOPS = 2 * K * N * (OWN_SLOTS + FAR_SLOTS)
 
 
 def tile_moe_loc_lin_relu_kernel(
@@ -36,107 +48,119 @@ def tile_moe_loc_lin_relu_kernel(
         reuse = ctx.enter_context(tc.tile_pool(name="reuse", bufs=1))
         psum = ctx.enter_context(tc.psum_pool(name="psum", bufs=1))
         banks = [psum.tile([P, BANK], F32, name=f"bank{b}") for b in range(8)]
+
+        def sbuf_tile(shape, dtype, name, at=None, align_bytes=None):
+            pool = keep if at is None else reuse
+            return pool.tile(shape, dtype, name=name, offset=at, align_bytes=align_bytes)
+
+        far_scale_table = keep.tile([P, WINDOW], U8, name="far_scale_table")
+        nc.gpsimd.memset(far_scale_table[:].bitcast(I32), 0)
+        far_word_table = keep.tile([P, WINDOW], I32, name="far_word_table")
+        nc.gpsimd.memset(far_word_table[:, FAR_TOKENS:], 0)
+        token_table = [keep.tile([P, 2 * WINDOW], BF16, name=f"token_table{u}") for u in range(2)]
+        for u in range(2):
+            nc.gpsimd.memset(token_table[u][:, 2 * OWN_TOKENS :].bitcast(I32), 0)
         identity = keep.tile([P, P], F32, name="identity")
+        make_identity(nc, identity[:])
+
+        xo_rows = xo.rearrange("(p j) t -> p j t", j=PACK)
+        xo_raw = [keep.tile([P, 2, OWN_TOKENS], F32, name=f"xo_raw{u}") for u in range(2)]
+        whole_raw = [keep.tile([P, PACK, N], F32, name=f"whole_raw{e}") for e in range(WHOLE_EXPERTS)]
+        w_raw = {}
+        for e in range(EXPERTS):
+            for h in range(2):
+                if e < WHOLE_EXPERTS:
+                    w_raw[e, h] = whole_raw[e][:, :, HALF * h : HALF * (h + 1)]
+                else:
+                    at = LAST_RAW_AT[h] if e == EXPERTS - 1 else None
+                    w_raw[e, h] = sbuf_tile([P, PACK, HALF], F32, f"w_raw{e}_{h}", at)[:]
+        gates = keep.tile([P, TOP, OWN_TOKENS], F32, name="gates")
 
         def load_list(src, name):
             tile = keep.tile([P, src.shape[1]], U16, name=name)
             nc.sync.dma_start(tile[:], src)
             return tile
 
-        far_scale_table = keep.tile([P, WINDOW], U8, name="far_scale_table")
-        nc.gpsimd.memset(far_scale_table[:].bitcast(I32), 0)
-        warm = keep.tile([P, 16], F32, name="warm")
-        nc.gpsimd.memset(warm[:, 0:1], 0.0)
-        far_word_table = keep.tile([P, WINDOW], I32, name="far_word_table")
-        nc.gpsimd.memset(far_word_table[:, Q:], 0)
-        pairs = [keep.tile([P, 2 * WINDOW], BF16, name=f"pairs{u}") for u in range(2)]
-        for u in range(2):
-            nc.gpsimd.memset(pairs[u][:, 2 * T :].bitcast(I32), 0)
-        make_identity(nc, identity[:])
-        xo_rows = xo.rearrange("(p j) t -> p j t", j=PACK)
-        xo_raw = [keep.tile([P, 2, T], F32, name=f"xo_raw{u}") for u in range(2)]
-        w_raw = {}
-        whole_raw = [keep.tile([P, PACK, N], F32, name=f"whole_raw{e}") for e in range(3)]
-        for e in range(3):
-            for h in range(2):
-                w_raw[e, h] = whole_raw[e][:, :, HALF * h : HALF * (h + 1)]
-        placed = {(5, 0): 5632, (5, 1): 15360 + 4096}
-        for e in range(3, E):
-            for h in range(2):
-                if (e, h) in placed:
-                    w_raw[e, h] = reuse.tile([P, PACK, HALF], F32, name=f"w_raw{e}_{h}", offset=placed[e, h])[:]
-                else:
-                    w_raw[e, h] = keep.tile([P, PACK, HALF], F32, name=f"w_raw{e}_{h}")[:]
+        def load_tokens(u, tokens):
+            nc.sync.dma_start(xo_raw[u][:, :, tokens], xo_rows[:, 2 * u : 2 * u + 2, tokens])
+
+        def load_scale_rows(q):
+            nc.sync.dma_start(
+                far_scale_table[32 * q : 32 * q + 4, :FAR_TOKENS].bitcast(I32),
+                x_scales[0, 4 * q : 4 * q + 4, :].bitcast(I32),
+            )
 
         def w_rows(e):
             return w[e].rearrange("(p j) n -> p j n", j=PACK)
 
-        def load_scale_rows(q):
-            nc.sync.dma_start(
-                far_scale_table[32 * q : 32 * q + 4, :Q].bitcast(I32), x_scales[0, 4 * q : 4 * q + 4, :].bitcast(I32)
-            )
-
         def load_half(e, h):
             nc.sync.dma_start(w_raw[e, h], w_rows(e)[:, :, HALF * h : HALF * (h + 1)])
 
-        nc.scalar.activation(warm[:, 8:9], warm[:, 0:1], RELU)
-        nc.sync.dma_start(far_word_table[:, :Q], x_words[0].rearrange("p t d -> p (t d)").bitcast(I32))
+        token_pieces = (slice(0, OWN_TOKENS // 2), slice(OWN_TOKENS // 2, OWN_TOKENS))
+        all_tokens = slice(0, OWN_TOKENS)
+        nc.sync.dma_start(far_word_table[:, :FAR_TOKENS], x_words[0].rearrange("p t d -> p (t d)").bitcast(I32))
         far_list = load_list(offs2, "far_list")
-        nc.sync.dma_start(xo_raw[0][:], xo_rows[:, 0:2, :])
+        for tokens in token_pieces:
+            load_tokens(0, tokens)
         own_list = load_list(offs, "own_list")
-        nc.sync.dma_start(xo_raw[1][:], xo_rows[:, 2:4, :])
-        load_half(3, 0)
-        nc.sync.dma_start(whole_raw[2][:], w_rows(2))
-        load_scale_rows(0)
-        load_scale_rows(1)
-        nc.sync.dma_start(whole_raw[0][:], w_rows(0))
-        load_scale_rows(2)
-        load_scale_rows(3)
-        nc.sync.dma_start(whole_raw[1][:], w_rows(1))
+        load_tokens(1, all_tokens)
+        for e in range(WHOLE_EXPERTS):
+            nc.sync.dma_start(whole_raw[e][:], w_rows(e))
+            load_scale_rows(2 * e)
+            load_scale_rows(2 * e + 1)
         slot_lists = [load_list(src, f"slot_list{r}") for r, src in enumerate((pos1, pos2, pos3))]
-        load_half(4, 0)
-        load_half(5, 0)
-        gates = keep.tile([P, TOP, T], F32, name="gates")
+        for e in range(WHOLE_EXPERTS, EXPERTS):
+            load_half(e, 0)
         nc.sync.dma_start(gates[:], gate.rearrange("r p t -> p r t"))
-        load_half(3, 1)
-        load_half(4, 1)
-        load_half(5, 1)
+        for e in range(WHOLE_EXPERTS, EXPERTS):
+            load_half(e, 1)
 
-        picked = keep.tile([P, 2, 2 * S], BF16, name="picked")
-        own_codes = keep.tile([P, S], U32, name="own_codes", align_bytes=64)
-        own_scales = keep.tile([P, S], U8, name="own_scales", align_bytes=64)
-        far_codes = keep.tile([P, R], U32, name="far_codes", align_bytes=64)
-        far_scales = reuse.tile([P, R], U8, name="far_scales", offset=6144, align_bytes=64)
-        w_codes = [keep.tile([P, E * HALF], U32, name=f"w_codes{h}", align_bytes=64) for h in range(2)]
-        w_scales = [keep.tile([P, E * HALF], U8, name=f"w_scales{h}", align_bytes=64) for h in range(2)]
-        y = [reuse.tile([P, S], F32, name=f"y{c}", offset=at) for c, at in enumerate((0, 9216, 15360, 21504))]
-        z = [keep.tile([P, 2, R], F32, name=f"z{h}") for h in range(2)]
+        picked = keep.tile([P, 2, 2 * OWN_SLOTS], BF16, name="picked")
+        own_rounded = keep.tile([P, PACK * OWN_SLOTS], BF16, name="own_rounded", align_bytes=64)
+        own_codes = keep.tile([P, OWN_SLOTS], U32, name="own_codes", align_bytes=64)
+        own_scales = keep.tile([P, OWN_SLOTS], U8, name="own_scales", align_bytes=64)
+        far_codes = keep.tile([P, FAR_SLOTS], U32, name="far_codes", align_bytes=64)
+        far_scales = sbuf_tile([P, FAR_SLOTS], U8, "far_scales", FAR_SCALES_AT, 64)
+        w_rounded = {}
+        for h in range(2):
+            for g in range(PAIRS):
+                at = LAST_ROUNDED_AT if (h, g) == (1, PAIRS - 1) else None
+                w_rounded[h, g] = sbuf_tile([P, 2 * PACK * HALF], BF16, f"w_rounded{h}_{g}", at, 64)
+        w_codes = [keep.tile([P, EXPERTS * HALF], U32, name=f"w_codes{h}", align_bytes=64) for h in range(2)]
+        w_scales = [keep.tile([P, EXPERTS * HALF], U8, name=f"w_scales{h}", align_bytes=64) for h in range(2)]
+        own_result = [sbuf_tile([P, OWN_SLOTS], F32, f"own_result{c}", RESULT_AT[c]) for c in range(CHUNKS)]
+        far_result = [keep.tile([P, 2, FAR_SLOTS], F32, name=f"far_result{h}") for h in range(2)]
+        turned = [sbuf_tile([P, OWN_TOKENS], F32, f"turned{c}", PARTIAL_AT if c == 2 else None) for c in range(3)]
+        totals = [keep.tile([P, OWN_TOKENS], F32, name=f"total{c}") for c in range(CHUNKS)]
+        terms = {}
 
-        def gather_far(dst, table, a, b):
-            nc.vector.tensor_copy(dst, table.indirect(far_list[:, a // 16 : b // 16]))
+        def token_views(u, tokens):
+            dst = token_table[u][:, 2 * tokens.start : 2 * tokens.stop].rearrange("p (t i) -> p t i", i=2)
+            return dst, xo_raw[u][:, :, tokens].rearrange("p i t -> p t i")
 
-        def round_tokens(u):
+        def round_w(e, h):
+            dst = w_rounded[h, e // 2][:, PACK * HALF * (e % 2) : PACK * HALF * (e % 2 + 1)]
             nc.scalar.copy(
-                pairs[u][:, : 2 * T].rearrange("p (t e) -> p t e", e=2), xo_raw[u][:].rearrange("p e t -> p t e")
+                dst.rearrange("p (c i j) -> p c j i", i=4, j=PACK),
+                w_raw[e, h].rearrange("p j (c i) -> p c j i", i=4),
+            )
+
+        def quantize_w(h, g):
+            cols = slice(2 * HALF * g, 2 * HALF * (g + 1))
+            nc.vector.quantize_mx(
+                out=w_codes[h][:, cols].bitcast(FP8X4), scales=w_scales[h][:, cols], in_=w_rounded[h, g][:]
             )
 
         def gather_own(u, g):
             nc.vector.tensor_copy(
                 picked[:, u, 2 * BANK * g : 2 * BANK * (g + 1)].bitcast(U32),
-                pairs[u][:].bitcast(U32).indirect(own_list[:, g * BANK // 16 : (g + 1) * BANK // 16]),
+                token_table[u][:].bitcast(U32).indirect(own_list[:, g * BANK // 16 : (g + 1) * BANK // 16]),
             )
 
-        grouped = keep.tile([P, PACK * S], BF16, name="grouped", align_bytes=64)
-        w_grouped = {}
-        for h in range(2):
-            for g in range(E // 2):
-                at = 27648 if (h, g) == (1, 2) else None
-                pool = keep if at is None else reuse
-                w_grouped[h, g] = pool.tile([P, 2 * PACK * HALF], BF16, name=f"w_grouped{h}_{g}", align_bytes=64, offset=at)
-
         def interleave_own(g):
+            dst = own_rounded[:, PACK * BANK * g : PACK * BANK * (g + 1)]
             nc.vector.tensor_copy(
-                grouped[:, PACK * BANK * g : PACK * BANK * (g + 1)].bitcast(I32).rearrange("p (s u) -> p s u", u=2),
+                dst.bitcast(I32).rearrange("p (s u) -> p s u", u=2),
                 picked[:, :, 2 * BANK * g : 2 * BANK * (g + 1)].bitcast(I32).rearrange("p u s -> p s u"),
             )
 
@@ -145,21 +169,7 @@ def tile_moe_loc_lin_relu_kernel(
             nc.vector.quantize_mx(
                 out=own_codes[:, cols].bitcast(FP8X4),
                 scales=own_scales[:, cols],
-                in_=grouped[:, PACK * BANK * g : PACK * BANK * (g + 1)],
-            )
-
-        def round_w(e, h):
-            nc.scalar.copy(
-                w_grouped[h, e // 2][:, PACK * HALF * (e % 2) : PACK * HALF * (e % 2 + 1)].rearrange("p (c i j) -> p c j i", i=4, j=PACK),
-                w_raw[e, h].rearrange("p j (c i) -> p c j i", i=4),
-            )
-
-        def quantize_w(h, g):
-            cols = slice(2 * HALF * g, 2 * HALF * (g + 1))
-            nc.vector.quantize_mx(
-                out=w_codes[h][:, cols].bitcast(FP8X4),
-                scales=w_scales[h][:, cols],
-                in_=w_grouped[h, g][:],
+                in_=own_rounded[:, PACK * BANK * g : PACK * BANK * (g + 1)],
             )
 
         def product(dst, e, c, codes, scales):
@@ -175,115 +185,114 @@ def tile_moe_loc_lin_relu_kernel(
                 stop=True,
             )
 
-        def own_results(c, g):
-            acc = banks[3 * (c % 2) + g]
+        def own_products(c, g):
+            bank = banks[PAIRS * (c % 2) + g]
             for i in range(2):
-                e = 2 * g + i
-                slots = slice(C * e, C * (e + 1))
-                product(acc[:, C * i : C * (i + 1)], e, c, own_codes[:, slots], own_scales[:, slots])
-            nc.scalar.activation(y[c][:, BANK * g : BANK * (g + 1)], acc[:], RELU)
+                slots = slice(OWN_PER_EXPERT * (2 * g + i), OWN_PER_EXPERT * (2 * g + i + 1))
+                dst = bank[:, OWN_PER_EXPERT * i : OWN_PER_EXPERT * (i + 1)]
+                product(dst, 2 * g + i, c, own_codes[:, slots], own_scales[:, slots])
+            nc.scalar.activation(own_result[c][:, BANK * g : BANK * (g + 1)], bank[:], RELU)
 
-        def far_results(h, g):
-            acc = banks[(6 + 3 * h + g) % 8][:].rearrange("p (k s) -> p k s", k=2)
+        def far_products(h, g, bank):
+            acc = bank[:].rearrange("p (k s) -> p k s", k=2)
             for k in range(2):
                 for i in range(2):
-                    e = 2 * g + i
-                    slots = slice(D * e, D * (e + 1))
-                    product(acc[:, k, D * i : D * (i + 1)], e, 2 * h + k, far_codes[:, slots], far_scales[:, slots])
-            nc.scalar.activation(z[h][:, :, 2 * D * g : 2 * D * (g + 1)], acc, RELU)
+                    slots = slice(FAR_PER_EXPERT * (2 * g + i), FAR_PER_EXPERT * (2 * g + i + 1))
+                    dst = acc[:, k, FAR_PER_EXPERT * i : FAR_PER_EXPERT * (i + 1)]
+                    product(dst, 2 * g + i, 2 * h + k, far_codes[:, slots], far_scales[:, slots])
+            nc.scalar.activation(far_result[h][:, :, 2 * FAR_PER_EXPERT * g : 2 * FAR_PER_EXPERT * (g + 1)], acc, RELU)
 
         def store_far(h):
             for k in range(2):
                 c = 2 * h + k
-                nc.sync.dma_start(out[P * c : P * (c + 1), T:], z[h][:, k, :])
+                nc.sync.dma_start(out[P * c : P * (c + 1), OWN_TOKENS:], far_result[h][:, k, :])
 
-        def weighted(c, cols):
-            width = cols.stop - cols.start
-            terms = []
+        def gather_terms(c):
             for r in range(TOP):
-                at = 27648 + 2048 * (r - 1) if c == 1 and r > 0 else None
-                pool = keep if at is None else reuse
-                term = pool.tile([P, width], F32, name=f"term{c}_{r}_{cols.start}", offset=at)
-                offsets = slot_lists[r][:, cols.start // 16 : cols.stop // 16]
-                nc.vector.tensor_tensor(term[:], y[c][:].indirect(offsets), gates[:, r, cols], MULT)
-                terms.append(term)
-            return terms
+                at = LAST_ROUNDED_AT + 4 * OWN_TOKENS * (r - 1) if c == 1 and r > 0 else None
+                terms[c, r] = sbuf_tile([P, OWN_TOKENS], F32, f"term{c}_{r}", at)
+                nc.vector.tensor_tensor(terms[c, r][:], own_result[c][:].indirect(slot_lists[r][:]), gates[:, r, :], MULT)
 
-        totals = [keep.tile([P, T], F32, name=f"total{c}") for c in range(CHUNKS)]
-        staged = [keep.tile([P, T], F32, name=f"staged{c}") for c in range(CHUNKS)]
-
-        def turn_and_add(c, terms, bank):
-            width = terms[0].shape[1]
-            for b in range(0, width, P):
+        def turn_and_add(c):
+            bank = banks[6]
+            for b in range(0, OWN_TOKENS, P):
                 for r in range(TOP):
                     nc.tensor.matmul(
                         bank[:, b : b + P],
-                        lhsT=terms[r][:, b : b + P],
+                        lhsT=terms[c, r][:, b : b + P],
                         rhs=identity[:],
                         start=r == 0,
                         stop=r == TOP - 1,
                         is_transpose=True,
                     )
-            nc.scalar.copy(staged[c][:, :width], bank[:, :width])
-
-        def turn_back(c, width, bank):
-            for b in range(0, width, P):
-                nc.tensor.transpose(bank[:, b : b + P], staged[c][:, b : b + P], identity[:])
-            nc.scalar.copy(totals[c][:, :width], bank[:, :width])
+            nc.scalar.copy(turned[c][:], bank[:])
 
         def store_own(c):
-            nc.sync.dma_start(out[P * c : P * (c + 1), :T], totals[c][:])
+            nc.sync.dma_start(out[P * c : P * (c + 1), :OWN_TOKENS], totals[c][:])
 
+        def turn_back(c, bank):
+            for b in range(0, OWN_TOKENS, P):
+                nc.tensor.transpose(bank[:, b : b + P], turned[c][:, b : b + P], identity[:])
+            nc.scalar.copy(totals[c][:], bank[:])
+            store_own(c)
+
+        nc.scalar.activation(*token_views(0, token_pieces[0]), COPY)
+        nc.scalar.copy(*token_views(0, token_pieces[1]))
+        nc.scalar.copy(*token_views(1, all_tokens))
+        for e in range(EXPERTS):
+            round_w(e, 0)
+            if e < WHOLE_EXPERTS:
+                round_w(e, 1)
+
+        nc.vector.tensor_copy(far_codes[:], far_word_table[:].bitcast(U32).indirect(far_list[:]))
         for u in range(2):
-            round_tokens(u)
-        for e, h in ((3, 0), (2, 0), (2, 1), (0, 0), (0, 1), (1, 0), (1, 1), (4, 0), (5, 0)):
-            round_w(e, h)
-        gather_far(far_codes[:], far_word_table[:].bitcast(U32), 0, R)
-        gather_own(0, 0)
-        gather_own(1, 0)
-        gather_own(0, 1)
-        interleave_own(0)
-        gather_own(1, 1)
-        quantize_own(0)
-        gather_own(0, 2)
-        interleave_own(1)
-        gather_own(1, 2)
-        quantize_own(1)
-        interleave_own(2)
+            gather_own(u, 0)
+        for g in range(1, PAIRS):
+            gather_own(0, g)
+            interleave_own(g - 1)
+            gather_own(1, g)
+            quantize_own(g - 1)
+        interleave_own(PAIRS - 1)
         quantize_w(0, 0)
-        quantize_own(2)
-        for g in range(1, E // 2):
+        quantize_own(PAIRS - 1)
+        for g in range(1, PAIRS):
             quantize_w(0, g)
-        gather_far(far_scales[:], far_scale_table[:], 0, R)
-        for c, g in ((0, 1), (0, 0), (0, 2), (1, 1), (1, 0)):
-            own_results(c, g)
-        for e in range(3, E - 1):
-            round_w(e, 1)
-        own_results(1, 2)
-        round_w(E - 1, 1)
-        for g in range(E // 2):
+        nc.vector.tensor_copy(far_scales[:], far_scale_table[:].indirect(far_list[:]))
+
+        for c, g in ((0, 0), (1, 0), (0, 1), (0, 2), (1, 1)):
+            own_products(c, g)
+        round_w(2, 1)
+        round_w(3, 1)
+        own_products(1, 2)
+        round_w(4, 1)
+        round_w(5, 1)
+        for g in range(PAIRS):
             quantize_w(1, g)
-        for c, g in ((2, 0), (2, 1), (3, 0), (3, 1), (2, 2), (3, 2)):
-            own_results(c, g)
-        for h in range(2):
-            for g in range(E // 2):
-                far_results(h, g)
-            store_far(h)
-        terms = [weighted(c, slice(0, T)) for c in range(CHUNKS - 1)]
-        terms.append(weighted(CHUNKS - 1, slice(0, T // 2)))
-        last = weighted(CHUNKS - 1, slice(T // 2, T))
-        turn_and_add(0, terms[0], banks[4])
-        turn_and_add(1, terms[1], banks[5])
-        turn_back(0, T, banks[6])
-        store_own(0)
-        turn_back(1, T, banks[7])
-        store_own(1)
-        turn_and_add(2, terms[2], banks[4])
-        turn_and_add(3, terms[3], banks[5])
-        turn_back(2, T, banks[2])
-        store_own(2)
-        turn_back(3, T // 2, banks[3])
-        partial = keep.tile([P, T // 2], F32, name="partial")
-        nc.vector.tensor_tensor(partial[:], last[0][:], last[1][:], ADD)
-        nc.vector.tensor_tensor(totals[3][:, T // 2 :], partial[:], last[2][:], ADD)
+        gather_terms(0)
+        gather_terms(1)
+
+        own_products(2, 0)
+        own_products(2, 1)
+        far_products(0, 0, banks[7])
+        turn_and_add(0)
+        own_products(2, 2)
+        gather_terms(2)
+        for g in range(PAIRS):
+            own_products(3, g)
+        gather_terms(3)
+        far_products(0, 1, banks[0])
+        far_products(0, 2, banks[1])
+        store_far(0)
+        turn_back(0, banks[7])
+        turn_and_add(1)
+        for g in range(PAIRS):
+            far_products(1, g, banks[2 + g])
+        store_far(1)
+        turn_and_add(2)
+        turn_back(1, banks[5])
+        turn_back(2, banks[7])
+
+        partial = sbuf_tile([P, OWN_TOKENS], F32, "partial", PARTIAL_AT)
+        nc.vector.tensor_tensor(partial[:], terms[3, 0][:], terms[3, 1][:], ADD)
+        nc.vector.tensor_tensor(totals[3][:], partial[:], terms[3, 2][:], ADD)
         store_own(3)

from contextlib import ExitStack

import concourse.mybir as mybir
from concourse.masks import make_identity

F32 = mybir.dt.float32
BF16 = mybir.dt.bfloat16
I32 = mybir.dt.int32
U32 = mybir.dt.uint32
U16 = mybir.dt.uint16
U8 = mybir.dt.uint8
FP8X4 = mybir.dt.float8_e4m3fn_x4
COPY = mybir.ActivationFunctionType.Copy
RELU = mybir.ActivationFunctionType.Relu
MULT = mybir.AluOpType.mult
ADD = mybir.AluOpType.add

K, N, EXPERTS, TOP = 512, 512, 6, 3
OWN_TOKENS, FAR_TOKENS = 512, 768
OWN_PER_EXPERT, FAR_PER_EXPERT = 256, 128
OWN_SLOTS, FAR_SLOTS = EXPERTS * OWN_PER_EXPERT, EXPERTS * FAR_PER_EXPERT
P = 128
PACK = 4
CHUNKS = N // P
HALF = N // 2
PAIRS = EXPERTS // 2
BANK = 512
WINDOW = 1024
WHOLE_EXPERTS = 2

RESULT_BYTES = 4 * OWN_SLOTS
SCALE_GAP = 3072
RESULT_AT = (0, RESULT_BYTES + SCALE_GAP, 2 * RESULT_BYTES + SCALE_GAP, 3 * RESULT_BYTES + SCALE_GAP)
FAR_SCALES_AT = RESULT_BYTES
LAST_RAW_AT = (RESULT_BYTES - 512, RESULT_AT[3] - 2048)
LAST_ROUNDED_AT = RESULT_AT[3] + RESULT_BYTES
PARTIAL_AT = LAST_ROUNDED_AT + 4096

FLOPS = 2 * K * N * (OWN_SLOTS + FAR_SLOTS)


def tile_moe_loc_lin_relu_kernel(
    tc, x_words, x_scales, xo, w, gate, offs, pos1, pos2, pos3, offs2, out
):
    nc = tc.nc
    with ExitStack() as ctx:
        keep = ctx.enter_context(tc.tile_pool(name="keep", bufs=1))
        reuse = ctx.enter_context(tc.tile_pool(name="reuse", bufs=1))
        psum = ctx.enter_context(tc.psum_pool(name="psum", bufs=1))
        banks = [psum.tile([P, BANK], F32, name=f"bank{b}") for b in range(8)]

        def sbuf_tile(shape, dtype, name, at=None, align_bytes=None):
            pool = keep if at is None else reuse
            return pool.tile(shape, dtype, name=name, offset=at, align_bytes=align_bytes)

        far_scale_table = keep.tile([P, WINDOW], U8, name="far_scale_table")
        nc.gpsimd.memset(far_scale_table[:].bitcast(I32), 0)
        far_word_table = keep.tile([P, WINDOW], I32, name="far_word_table")
        nc.gpsimd.memset(far_word_table[:, FAR_TOKENS:], 0)
        token_table = [keep.tile([P, 2 * WINDOW], BF16, name=f"token_table{u}") for u in range(2)]
        for u in range(2):
            nc.gpsimd.memset(token_table[u][:, 2 * OWN_TOKENS :].bitcast(I32), 0)
        identity = keep.tile([P, P], F32, name="identity")
        make_identity(nc, identity[:])

        xo_rows = xo.rearrange("(p j) t -> p j t", j=PACK)
        xo_raw = [keep.tile([P, 2, OWN_TOKENS], F32, name=f"xo_raw{u}") for u in range(2)]
        whole_raw = [keep.tile([P, PACK, N], F32, name=f"whole_raw{e}") for e in range(WHOLE_EXPERTS)]
        w_raw = {}
        for e in range(EXPERTS):
            for h in range(2):
                if e < WHOLE_EXPERTS:
                    w_raw[e, h] = whole_raw[e][:, :, HALF * h : HALF * (h + 1)]
                else:
                    at = LAST_RAW_AT[h] if e == EXPERTS - 1 else None
                    w_raw[e, h] = sbuf_tile([P, PACK, HALF], F32, f"w_raw{e}_{h}", at)[:]
        gates = keep.tile([P, TOP, OWN_TOKENS], F32, name="gates")

        def load_list(src, name):
            tile = keep.tile([P, src.shape[1]], U16, name=name)
            nc.sync.dma_start(tile[:], src)
            return tile

        def load_tokens(u, tokens):
            nc.sync.dma_start(xo_raw[u][:, :, tokens], xo_rows[:, 2 * u : 2 * u + 2, tokens])

        def load_scale_rows(q):
            nc.sync.dma_start(
                far_scale_table[32 * q : 32 * q + 4, :FAR_TOKENS].bitcast(I32),
                x_scales[0, 4 * q : 4 * q + 4, :].bitcast(I32),
            )

        def w_rows(e):
            return w[e].rearrange("(p j) n -> p j n", j=PACK)

        def load_half(e, h):
            nc.sync.dma_start(w_raw[e, h], w_rows(e)[:, :, HALF * h : HALF * (h + 1)])

        token_pieces = (slice(0, OWN_TOKENS // 2), slice(OWN_TOKENS // 2, OWN_TOKENS))
        all_tokens = slice(0, OWN_TOKENS)
        nc.sync.dma_start(far_word_table[:, :FAR_TOKENS], x_words[0].rearrange("p t d -> p (t d)").bitcast(I32))
        far_list = load_list(offs2, "far_list")
        for tokens in token_pieces:
            load_tokens(0, tokens)
        own_list = load_list(offs, "own_list")
        load_tokens(1, all_tokens)
        for e in range(WHOLE_EXPERTS):
            nc.sync.dma_start(whole_raw[e][:], w_rows(e))
            load_scale_rows(2 * e)
            load_scale_rows(2 * e + 1)
        slot_lists = [load_list(src, f"slot_list{r}") for r, src in enumerate((pos1, pos2, pos3))]
        for e in range(WHOLE_EXPERTS, EXPERTS):
            load_half(e, 0)
        nc.sync.dma_start(gates[:], gate.rearrange("r p t -> p r t"))
        for e in range(WHOLE_EXPERTS, EXPERTS):
            load_half(e, 1)

        picked = keep.tile([P, 2, 2 * OWN_SLOTS], BF16, name="picked")
        own_rounded = keep.tile([P, PACK * OWN_SLOTS], BF16, name="own_rounded", align_bytes=64)
        own_codes = keep.tile([P, OWN_SLOTS], U32, name="own_codes", align_bytes=64)
        own_scales = keep.tile([P, OWN_SLOTS], U8, name="own_scales", align_bytes=64)
        far_codes = keep.tile([P, FAR_SLOTS], U32, name="far_codes", align_bytes=64)
        far_scales = sbuf_tile([P, FAR_SLOTS], U8, "far_scales", FAR_SCALES_AT, 64)
        w_rounded = {}
        for h in range(2):
            for g in range(PAIRS):
                at = LAST_ROUNDED_AT if (h, g) == (1, PAIRS - 1) else None
                w_rounded[h, g] = sbuf_tile([P, 2 * PACK * HALF], BF16, f"w_rounded{h}_{g}", at, 64)
        w_codes = [keep.tile([P, EXPERTS * HALF], U32, name=f"w_codes{h}", align_bytes=64) for h in range(2)]
        w_scales = [keep.tile([P, EXPERTS * HALF], U8, name=f"w_scales{h}", align_bytes=64) for h in range(2)]
        own_result = [sbuf_tile([P, OWN_SLOTS], F32, f"own_result{c}", RESULT_AT[c]) for c in range(CHUNKS)]
        far_result = [keep.tile([P, 2, FAR_SLOTS], F32, name=f"far_result{h}") for h in range(2)]
        turned = [sbuf_tile([P, OWN_TOKENS], F32, f"turned{c}", PARTIAL_AT if c == 2 else None) for c in range(3)]
        totals = [keep.tile([P, OWN_TOKENS], F32, name=f"total{c}") for c in range(CHUNKS)]
        terms = {}

        def token_views(u, tokens):
            dst = token_table[u][:, 2 * tokens.start : 2 * tokens.stop].rearrange("p (t i) -> p t i", i=2)
            return dst, xo_raw[u][:, :, tokens].rearrange("p i t -> p t i")

        def round_w(e, h):
            dst = w_rounded[h, e // 2][:, PACK * HALF * (e % 2) : PACK * HALF * (e % 2 + 1)]
            nc.scalar.copy(
                dst.rearrange("p (c i j) -> p c j i", i=4, j=PACK),
                w_raw[e, h].rearrange("p j (c i) -> p c j i", i=4),
            )

        def quantize_w(h, g):
            cols = slice(2 * HALF * g, 2 * HALF * (g + 1))
            nc.vector.quantize_mx(
                out=w_codes[h][:, cols].bitcast(FP8X4), scales=w_scales[h][:, cols], in_=w_rounded[h, g][:]
            )

        def gather_own(u, g):
            nc.vector.tensor_copy(
                picked[:, u, 2 * BANK * g : 2 * BANK * (g + 1)].bitcast(U32),
                token_table[u][:].bitcast(U32).indirect(own_list[:, g * BANK // 16 : (g + 1) * BANK // 16]),
            )

        def interleave_own(g):
            dst = own_rounded[:, PACK * BANK * g : PACK * BANK * (g + 1)]
            nc.vector.tensor_copy(
                dst.bitcast(I32).rearrange("p (s u) -> p s u", u=2),
                picked[:, :, 2 * BANK * g : 2 * BANK * (g + 1)].bitcast(I32).rearrange("p u s -> p s u"),
            )

        def quantize_own(g):
            cols = slice(BANK * g, BANK * (g + 1))
            nc.vector.quantize_mx(
                out=own_codes[:, cols].bitcast(FP8X4),
                scales=own_scales[:, cols],
                in_=own_rounded[:, PACK * BANK * g : PACK * BANK * (g + 1)],
            )

        def product(dst, e, c, codes, scales):
            h, k = divmod(c, 2)
            cols = slice(HALF * e + P * k, HALF * e + P * (k + 1))
            nc.tensor.matmul_mx(
                out=dst,
                lhsT=w_codes[h][:, cols].bitcast(FP8X4),
                lhsT_scale=w_scales[h][:, cols],
                rhs=codes.bitcast(FP8X4),
                rhs_scale=scales,
                start=True,
                stop=True,
            )

        def own_products(c, g):
            bank = banks[PAIRS * (c % 2) + g]
            for i in range(2):
                slots = slice(OWN_PER_EXPERT * (2 * g + i), OWN_PER_EXPERT * (2 * g + i + 1))
                dst = bank[:, OWN_PER_EXPERT * i : OWN_PER_EXPERT * (i + 1)]
                product(dst, 2 * g + i, c, own_codes[:, slots], own_scales[:, slots])
            nc.scalar.activation(own_result[c][:, BANK * g : BANK * (g + 1)], bank[:], RELU)

        def far_products(h, g, bank):
            acc = bank[:].rearrange("p (k s) -> p k s", k=2)
            for k in range(2):
                for i in range(2):
                    slots = slice(FAR_PER_EXPERT * (2 * g + i), FAR_PER_EXPERT * (2 * g + i + 1))
                    dst = acc[:, k, FAR_PER_EXPERT * i : FAR_PER_EXPERT * (i + 1)]
                    product(dst, 2 * g + i, 2 * h + k, far_codes[:, slots], far_scales[:, slots])
            nc.scalar.activation(far_result[h][:, :, 2 * FAR_PER_EXPERT * g : 2 * FAR_PER_EXPERT * (g + 1)], acc, RELU)

        def store_far(h):
            for k in range(2):
                c = 2 * h + k
                nc.sync.dma_start(out[P * c : P * (c + 1), OWN_TOKENS:], far_result[h][:, k, :])

        def gather_terms(c):
            for r in range(TOP):
                at = LAST_ROUNDED_AT + 4 * OWN_TOKENS * (r - 1) if c == 1 and r > 0 else None
                terms[c, r] = sbuf_tile([P, OWN_TOKENS], F32, f"term{c}_{r}", at)
                nc.vector.tensor_tensor(terms[c, r][:], own_result[c][:].indirect(slot_lists[r][:]), gates[:, r, :], MULT)

        def turn_and_add(c):
            bank = banks[6]
            for b in range(0, OWN_TOKENS, P):
                for r in range(TOP):
                    nc.tensor.matmul(
                        bank[:, b : b + P],
                        lhsT=terms[c, r][:, b : b + P],
                        rhs=identity[:],
                        start=r == 0,
                        stop=r == TOP - 1,
                        is_transpose=True,
                    )
            nc.scalar.copy(turned[c][:], bank[:])

        def store_own(c):
            nc.sync.dma_start(out[P * c : P * (c + 1), :OWN_TOKENS], totals[c][:])

        def turn_back(c, bank):
            for b in range(0, OWN_TOKENS, P):
                nc.tensor.transpose(bank[:, b : b + P], turned[c][:, b : b + P], identity[:])
            nc.scalar.copy(totals[c][:], bank[:])
            store_own(c)

        nc.scalar.activation(*token_views(0, token_pieces[0]), COPY)
        nc.scalar.copy(*token_views(0, token_pieces[1]))
        nc.scalar.copy(*token_views(1, all_tokens))
        for e in range(EXPERTS):
            round_w(e, 0)
            if e < WHOLE_EXPERTS:
                round_w(e, 1)

        nc.vector.tensor_copy(far_codes[:], far_word_table[:].bitcast(U32).indirect(far_list[:]))
        for u in range(2):
            gather_own(u, 0)
        for g in range(1, PAIRS):
            gather_own(0, g)
            interleave_own(g - 1)
            gather_own(1, g)
            quantize_own(g - 1)
        interleave_own(PAIRS - 1)
        quantize_w(0, 0)
        quantize_own(PAIRS - 1)
        for g in range(1, PAIRS):
            quantize_w(0, g)
        nc.vector.tensor_copy(far_scales[:], far_scale_table[:].indirect(far_list[:]))

        for c, g in ((0, 0), (1, 0), (0, 1), (0, 2), (1, 1)):
            own_products(c, g)
        round_w(2, 1)
        round_w(3, 1)
        own_products(1, 2)
        round_w(4, 1)
        round_w(5, 1)
        for g in range(PAIRS):
            quantize_w(1, g)
        gather_terms(0)
        gather_terms(1)

        own_products(2, 0)
        own_products(2, 1)
        far_products(0, 0, banks[7])
        turn_and_add(0)
        own_products(2, 2)
        gather_terms(2)
        for g in range(PAIRS):
            own_products(3, g)
        gather_terms(3)
        far_products(0, 1, banks[0])
        far_products(0, 2, banks[1])
        store_far(0)
        turn_back(0, banks[7])
        turn_and_add(1)
        for g in range(PAIRS):
            far_products(1, g, banks[2 + g])
        store_far(1)
        turn_and_add(2)
        turn_back(1, banks[5])
        turn_back(2, banks[7])

        partial = sbuf_tile([P, OWN_TOKENS], F32, "partial", PARTIAL_AT)
        nc.vector.tensor_tensor(partial[:], terms[3, 0][:], terms[3, 1][:], ADD)
        nc.vector.tensor_tensor(totals[3][:], partial[:], terms[3, 2][:], ADD)
        store_own(3)
